import numpy as np
import ml_dtypes


def mxq(x, axis, fmt="e4m3"):
    dtype, down = {"e4m3": (ml_dtypes.float8_e4m3fn, 7), "e5m2": (ml_dtypes.float8_e5m2, 14)}[fmt]
    v = np.moveaxis(np.asarray(x, np.float32).astype(ml_dtypes.bfloat16).astype(np.float64), axis, -1)
    blocks = v.reshape(v.shape[:-1] + (-1, 32))
    amax = np.abs(blocks).max(-1, keepdims=True)
    byte = np.maximum(np.where(amax > 0, np.frexp(amax)[1] - 1 + 127, 0) - down, 1)
    scale = np.exp2(byte - 127.0)
    codes = (blocks / scale).astype(np.float32).astype(dtype).astype(np.float64)
    return np.moveaxis((codes * scale).reshape(v.shape), -1, axis)


WIDE = False


def mx_kscale(k):
    if not WIDE:
        return np.ones(k)
    levels = np.array([10, -10, 5, -5, 0])
    if k % 512:
        return np.exp2(np.random.permutation(np.resize(levels, k // 32))).repeat(32)
    a = np.empty((k // 512, 16))
    for p in range(k // 512):
        a[p, :8] = np.random.permutation(np.resize(levels, 8))
        for g in range(8):
            far = levels[np.abs(levels - a[p, g]) >= 10]
            a[p, g + 8] = far[np.random.randint(len(far))]
    return np.exp2(a.ravel()).repeat(32)


def f64(x):
    return np.asarray(x).astype(np.float64)


def striped(idx):
    return np.tile(idx.reshape(-1, 16).T, (8, 1)).astype(np.uint16)


def unstriped(offs):
    return offs[:16].T.reshape(-1).astype(np.int64)


def striped8(idx):
    return np.concatenate([v.reshape(-1, 16).T for v in idx]).astype(np.uint16)


def unstriped8(offs):
    return np.stack([offs[16 * g:16 * g + 16].T.reshape(-1) for g in range(8)]).astype(np.int64)


E2M1 = np.array([0.0, 0.5, 1.0, 1.5, 2.0, 3.0, 4.0, 6.0, -0.0, -0.5, -1.0, -1.5, -2.0, -3.0, -4.0, -6.0])


def pack_weight(w, fmt):
    k, n = w.shape
    w = f64(np.asarray(w, np.float32).astype(ml_dtypes.bfloat16)).reshape(k // 32, 32, n)
    amax = np.abs(w).max(1)
    if fmt == "e4m3":
        byte = np.frexp(amax)[1] - 1 + 127 - 7
    else:
        mant, ex = np.frexp(amax / 6.0)
        byte = np.where(mant > 0.5, ex, ex - 1) + 127
    byte = np.clip(np.where(amax > 0, byte, 1), 1, 254)
    scaled = (w * np.exp2(127.0 - byte)[:, None, :]).reshape(k, n).astype(np.float32)
    by_word = np.ascontiguousarray(scaled.reshape(k // 512, 128, 4, n).transpose(0, 1, 3, 2))
    if fmt == "e4m3":
        words = by_word.astype(ml_dtypes.float8_e4m3fn).view(np.uint8)
    else:
        c = by_word.astype(ml_dtypes.float4_e2m1fn).view(np.uint8) & 0xF
        words = (c[..., 0::2] | (c[..., 1::2] << 4)).reshape(k // 512, 128, 2 * n)
    return np.ascontiguousarray(words), np.ascontiguousarray(byte.astype(np.uint8).reshape(k // 512, 16, n))


def unpack_weight(words, scales, fmt):
    g, _, n = scales.shape
    words = np.ascontiguousarray(words).reshape(g, 128, n, -1)
    if fmt == "e4m3":
        vals = words.view(ml_dtypes.float8_e4m3fn).astype(np.float64)
    else:
        nib = np.empty((g, 128, n, 4), np.uint8)
        nib[..., 0::2] = words & 0xF
        nib[..., 1::2] = words >> 4
        vals = E2M1[nib]
    vals = vals * np.repeat(np.exp2(scales.astype(np.float64) - 127.0), 8, axis=1)[..., None]
    return vals.transpose(0, 1, 3, 2).reshape(g * 512, n)


def pack_table(v):
    words, scales = pack_weight(v, "e4m3")
    return np.concatenate([words.reshape(words.shape[0], -1), scales.reshape(scales.shape[0], -1)], axis=1)


def unpack_table(tab):
    g, t = tab.shape[0], tab.shape[1] // 528
    return unpack_weight(tab[:, :512 * t].reshape(g, 128, t, 4), tab[:, 512 * t:].reshape(g, 16, t), "e4m3")


def silu(v):
    return v / (1.0 + np.exp(-np.maximum(v, -700.0)))


K, M, T, S = 512, 512, 512, 256


def setup_inputs():
    n = np.random.standard_normal
    s = mx_kscale(K)[:, None]
    u = mx_kscale(512)[:, None]
    p_w2 = pack_weight(1.4 * n((512, M)) / np.sqrt(512) / u, "e2m1")
    return {
        "tab": pack_table(n((K, T)) * s),
        "w1": (n((K, 512)) / np.sqrt(K) / s * u.T).astype(np.float32),
        "w2_words": p_w2[0],
        "w2_scales": p_w2[1],
        "b": (0.3 * n(512)).astype(np.float32),
        "wgo": np.repeat(np.random.uniform(0.5, 2.0, (8, S)), 16, axis=0).astype(np.float32),
        "offs": striped(np.random.permutation(T)[:S]),
        "offs2": striped8(np.stack([np.random.permutation(T)[:S] for _ in range(8)])),
    }


def reference(tab, w1, w2_words, w2_scales, b, wgo, offs, offs2):
    tab_ = unpack_table(tab)[:, unstriped(offs)]
    w1_ = mxq(f64(w1), 0, "e4m3")
    w2_ = unpack_weight(w2_words, w2_scales, "e2m1")
    h_ = mxq(np.maximum(w1_.T @ tab_, 0.0), 0, "e4m3")
    y = w2_.T @ h_
    place = unstriped8(offs2)[np.arange(M) % 128 // 16]
    out = np.zeros((M, T))
    out[np.arange(M)[:, None], place] = f64(wgo)[np.arange(M) % 128] * (silu(y + f64(b)[:, None]))
    return out

@@ -1,0 +1,146 @@
+from contextlib import ExitStack
+
+import concourse.mybir as mybir
+
+K, R, M, T, S = 512, 512, 512, 512, 256
+FLOPS = 2 * K * R * S + 2 * R * M * S
+
+F32 = mybir.dt.float32
+BF16 = mybir.dt.bfloat16
+I32 = mybir.dt.int32
+U32 = mybir.dt.uint32
+U16 = mybir.dt.uint16
+U8 = mybir.dt.uint8
+FP8X4 = mybir.dt.float8_e4m3fn_x4
+FP4X4 = mybir.dt.float4_e2m1fn_x4
+ACT = mybir.ActivationFunctionType
+MULT = mybir.AluOpType.mult
+
+P = 128
+PACK = 4
+HALF = S // 2
+
+
+def load_scale_rows(nc, plane, rows):
+    for q in range(4):
+        nc.sync.dma_start(out=plane[32 * q : 32 * q + 4, :].bitcast(I32), in_=rows[4 * q : 4 * q + 4, :].bitcast(I32))
+
+
+def tile_list_tabhs_m_silu_kernel(tc, tab, w1, w2_words, w2_scales, b, wgo, offs, offs2, out):
+    nc = tc.nc
+    with ExitStack() as ctx:
+        sb = ctx.enter_context(tc.tile_pool(name="sb", bufs=1))
+        ps = ctx.enter_context(tc.psum_pool(name="ps", bufs=1))
+
+        pick = sb.tile([P, S // 16], U16, name="pick")
+        place = sb.tile([P, S // 16], U16, name="place")
+        tab_words = sb.tile([P, T], I32, name="tab_words", align_bytes=64)
+        tab_plane = sb.tile([P, T], U8, name="tab_plane", align_bytes=64)
+        w2_codes = sb.tile([P, 2 * M], U8, name="w2_codes", align_bytes=64)
+        w2_plane = sb.tile([P, M], U8, name="w2_plane", align_bytes=64)
+        bias = sb.tile([P, M // P], F32, name="bias")
+        gain = sb.tile([P, S], F32, name="gain")
+        zero_in = sb.tile([P, 1], F32, name="zero_in")
+        zero = sb.tile([P, 1], F32, name="zero")
+        pages = [sb.tile([P, T], F32, name="page%d" % c) for c in range(M // P)]
+
+        nc.gpsimd.memset(zero_in[:], 0.0)
+        nc.scalar.activation(out=zero[:], in_=zero_in[:], func=ACT.Silu)
+
+        nc.vector.memset(tab_plane[:].bitcast(I32), 0)
+        nc.vector.memset(w2_plane[:].bitcast(I32), 0)
+        for page in pages:
+            nc.vector.memset(page[:], 0.0)
+
+        nc.sync.dma_start(pick[:], offs)
+        nc.sync.dma_start(out=tab_words[:], in_=tab[0, 0 : 4 * P * T].rearrange("(p c) -> p c", p=P).bitcast(I32))
+        load_scale_rows(nc, tab_plane, tab[0, 4 * P * T :].rearrange("(q t) -> q t", t=T))
+        w1_rows = w1.rearrange("(p j) r -> p j r", j=PACK)
+        chunks = [(0, 256), (256, 384), (384, 512)]
+        raw = []
+        for lo, hi in chunks:
+            piece = sb.tile([P, PACK, hi - lo], F32, name="w1_raw%d" % lo)
+            nc.sync.dma_start(out=piece[:], in_=w1_rows[:, :, lo:hi])
+            raw.append(piece)
+        nc.sync.dma_start(out=w2_codes[:].bitcast(I32), in_=w2_words[0].bitcast(I32))
+        load_scale_rows(nc, w2_plane, w2_scales[0])
+        with nc.allow_non_contiguous_dma(reason="one bias value a partition and row block"):
+            nc.sync.dma_start(out=bias[:], in_=b.rearrange("(c p) -> p c", p=P))
+        nc.sync.dma_start(place[:], offs2)
+        nc.sync.dma_start(out=gain[:], in_=wgo)
+
+        v_words = sb.tile([P, S], U32, name="v_words", align_bytes=64)
+        v_plane = sb.tile([P, S], U8, name="v_plane", align_bytes=64)
+        nc.vector.tensor_copy(out=v_words[:], in_=tab_words[:].bitcast(U32).indirect(pick[:]))
+        nc.vector.tensor_copy(out=v_plane[:], in_=tab_plane[:].indirect(pick[:]))
+
+        grouped = [sb.tile([P, PACK, 64, PACK], BF16, name="w1_grouped%d" % u, align_bytes=64) for u in range(2)]
+        w1_codes = [sb.tile([P, P], U32, name="w1_codes%d" % t, align_bytes=64) for t in range(PACK)]
+        w1_plane = [sb.tile([P, P], U8, name="w1_plane%d" % t, align_bytes=64) for t in range(PACK)]
+
+        def views(piece, u, m0, m1):
+            src = piece[:].rearrange("p j (m t) -> p m j t", t=PACK)
+            dst = grouped[u][:, :, m0:m1, :].rearrange("p t m j -> p m j t")
+            return dst, src
+
+        def quantize_w1(u):
+            for t in range(PACK):
+                nc.vector.quantize_mx(
+                    out=w1_codes[t][:, 64 * u : 64 * u + 64].bitcast(FP8X4),
+                    scales=w1_plane[t][:, 64 * u : 64 * u + 64],
+                    in_=grouped[u][:, t, :, :].rearrange("p m j -> p (m j)"),
+                )
+
+        dst, src = views(raw[0], 0, 0, 64)
+        nc.vector.tensor_copy(out=dst, in_=src)
+        quantize_w1(0)
+        dst, src = views(raw[1], 1, 0, 32)
+        nc.scalar.copy(out=dst, in_=src)
+        dst, src = views(raw[2], 1, 32, 64)
+        nc.vector.tensor_copy(out=dst, in_=src)
+        quantize_w1(1)
+
+        h_codes = sb.tile([P, S], U32, name="h_codes", align_bytes=64)
+        h_plane = sb.tile([P, S], U8, name="h_plane", align_bytes=64)
+        for u in range(2):
+            cols = slice(u * HALF, (u + 1) * HALF)
+            h_sum = ps.tile([P, PACK, HALF], F32, name="h_sum%d" % u)
+            for t in range(PACK):
+                nc.tensor.matmul_mx(
+                    out=h_sum[:, t, :],
+                    lhsT=w1_codes[t][:].bitcast(FP8X4),
+                    lhsT_scale=w1_plane[t][:],
+                    rhs=v_words[:, cols].bitcast(FP8X4),
+                    rhs_scale=v_plane[:, cols],
+                    start=True,
+                    stop=True,
+                )
+            h_grouped = sb.tile([P, HALF, PACK], BF16, name="h_grouped%d" % u, align_bytes=64)
+            nc.scalar.activation(
+                out=h_grouped[:], in_=h_sum[:].rearrange("p t s -> p s t"), func=ACT.Relu, bias=zero[:]
+            )
+            nc.vector.quantize_mx(
+                out=h_codes[:, cols].bitcast(FP8X4),
+                scales=h_plane[:, cols],
+                in_=h_grouped[:].rearrange("p s t -> p (s t)"),
+            )
+
+        steps = [(0, 0, HALF), (1, 0, S), (0, HALF, S), (2, 0, S), (3, 0, S)]
+        for c, s0, s1 in steps:
+            y_sum = ps.tile([P, s1 - s0], F32, name="y_sum%d_%d" % (c, s0))
+            nc.tensor.matmul_mx(
+                out=y_sum[:],
+                lhsT=w2_codes[:, 2 * P * c : 2 * P * (c + 1)].bitcast(FP4X4),
+                lhsT_scale=w2_plane[:, P * c : P * (c + 1)],
+                rhs=h_codes[:, s0:s1].bitcast(FP8X4),
+                rhs_scale=h_plane[:, s0:s1],
+                start=True,
+                stop=True,
+            )
+            act = sb.tile([P, s1 - s0], F32, name="act%d_%d" % (c, s0))
+            nc.scalar.activation(out=act[:], in_=y_sum[:], func=ACT.Silu, bias=bias[:, c : c + 1])
+            nc.vector.tensor_tensor(
+                out=pages[c][:].indirect(place[:, s0 // 16 : s1 // 16]), in0=act[:], in1=gain[:, s0:s1], op=MULT
+            )
+            if s1 == S:
+                nc.sync.dma_start(out=out[P * c : P * (c + 1), :], in_=pages[c][:])

@@ -53,81 +53,104 @@ def tile_list_tabhs_m_silu_kernel(tc, tab, w1, w2_words, w2_scales, b, wgo, offs
             nc.vector.memset(page[:], 0.0)
 
         nc.sync.dma_start(pick[:], offs)
+        nc.sync.dma_start(place[:], offs2)
         nc.sync.dma_start(out=tab_words[:], in_=tab[0, 0 : 4 * P * T].rearrange("(p c) -> p c", p=P).bitcast(I32))
         load_scale_rows(nc, tab_plane, tab[0, 4 * P * T :].rearrange("(q t) -> q t", t=T))
         w1_rows = w1.rearrange("(p j) r -> p j r", j=PACK)
         chunks = [(0, 256), (256, 384), (384, 512)]
         raw = []
-        for lo, hi in chunks:
-            piece = sb.tile([P, PACK, hi - lo], F32, name="w1_raw%d" % lo)
+        for n, (lo, hi) in enumerate(chunks):
+            piece = sb.tile([P, PACK, hi - lo], F32, name="w1_raw%d" % n, tag="raw%d" % n, align_bytes=64)
             nc.sync.dma_start(out=piece[:], in_=w1_rows[:, :, lo:hi])
             raw.append(piece)
         nc.sync.dma_start(out=w2_codes[:].bitcast(I32), in_=w2_words[0].bitcast(I32))
         load_scale_rows(nc, w2_plane, w2_scales[0])
         with nc.allow_non_contiguous_dma(reason="one bias value a partition and row block"):
             nc.sync.dma_start(out=bias[:], in_=b.rearrange("(c p) -> p c", p=P))
-        nc.sync.dma_start(place[:], offs2)
         nc.sync.dma_start(out=gain[:], in_=wgo)
 
-        v_words = sb.tile([P, S], U32, name="v_words", align_bytes=64)
+        def gather_words(u, tag):
+            words = sb.tile([P, HALF], U32, name="v_words%d" % u, tag=tag, align_bytes=64)
+            entries = pick[:, u * HALF // 16 : (u + 1) * HALF // 16]
+            nc.vector.tensor_copy(out=words[:], in_=tab_words[:].bitcast(U32).indirect(entries))
+            return words
+
+        v_words = [gather_words(0, "v_words0")]
         v_plane = sb.tile([P, S], U8, name="v_plane", align_bytes=64)
-        nc.vector.tensor_copy(out=v_words[:], in_=tab_words[:].bitcast(U32).indirect(pick[:]))
         nc.vector.tensor_copy(out=v_plane[:], in_=tab_plane[:].indirect(pick[:]))
 
-        grouped = [sb.tile([P, PACK, 64, PACK], BF16, name="w1_grouped%d" % u, align_bytes=64) for u in range(2)]
+        low = sb.tile([P, PACK, 64, PACK], BF16, name="w1_low", align_bytes=64)
+        high = [sb.tile([P, 2, 64, PACK], BF16, name="w1_high%d" % e, tag="high%d" % e, align_bytes=64) for e in range(2)]
         w1_codes = [sb.tile([P, P], U32, name="w1_codes%d" % t, align_bytes=64) for t in range(PACK)]
         w1_plane = [sb.tile([P, P], U8, name="w1_plane%d" % t, align_bytes=64) for t in range(PACK)]
 
-        def views(piece, u, m0, m1):
-            src = piece[:].rearrange("p j (m t) -> p m j t", t=PACK)
-            dst = grouped[u][:, :, m0:m1, :].rearrange("p t m j -> p m j t")
-            return dst, src
+        def source(n, m0, m1, t0, t1):
+            return raw[n][:, :, PACK * m0 : PACK * m1].rearrange("p j (m t) -> p m t j", t=PACK)[:, :, t0:t1, :]
 
-        def quantize_w1(u):
-            for t in range(PACK):
-                nc.vector.quantize_mx(
-                    out=w1_codes[t][:, 64 * u : 64 * u + 64].bitcast(FP8X4),
-                    scales=w1_plane[t][:, 64 * u : 64 * u + 64],
-                    in_=grouped[u][:, t, :, :].rearrange("p m j -> p (m j)"),
-                )
+        def target(tile, m0, m1, t0, t1):
+            return tile[:, t0:t1, m0:m1, :].rearrange("p t m j -> p m t j")
 
-        dst, src = views(raw[0], 0, 0, 64)
-        nc.vector.tensor_copy(out=dst, in_=src)
-        quantize_w1(0)
-        dst, src = views(raw[1], 1, 0, 32)
-        nc.scalar.copy(out=dst, in_=src)
-        dst, src = views(raw[2], 1, 32, 64)
-        nc.vector.tensor_copy(out=dst, in_=src)
-        quantize_w1(1)
+        def quantize_w1(u, t, rows):
+            nc.vector.quantize_mx(
+                out=w1_codes[t][:, 64 * u : 64 * u + 64].bitcast(FP8X4),
+                scales=w1_plane[t][:, 64 * u : 64 * u + 64],
+                in_=rows.rearrange("p m j -> p (m j)"),
+            )
+
+        nc.vector.tensor_copy(out=target(low, 0, 40, 0, 4), in_=source(0, 0, 40, 0, 4))
+        nc.scalar.copy(out=target(low, 40, 64, 0, 4), in_=source(0, 40, 64, 0, 4))
+        for t in range(PACK):
+            quantize_w1(0, t, low[:, t, :, :])
+        for n in (1, 2):
+            m0 = 32 * (n - 1)
+            nc.vector.tensor_copy(out=target(high[0], m0, m0 + 32, 0, 2), in_=source(n, 0, 32, 0, 2))
+            nc.scalar.copy(out=target(high[1], m0, m0 + 32, 0, 2), in_=source(n, 0, 32, 2, 4))
+        for t in range(PACK):
+            quantize_w1(1, t, high[t // 2][:, t % 2, :, :])
+
+        v_words.append(gather_words(1, "high0"))
 
         h_codes = sb.tile([P, S], U32, name="h_codes", align_bytes=64)
         h_plane = sb.tile([P, S], U8, name="h_plane", align_bytes=64)
-        for u in range(2):
-            cols = slice(u * HALF, (u + 1) * HALF)
-            h_sum = ps.tile([P, PACK, HALF], F32, name="h_sum%d" % u)
-            for t in range(PACK):
-                nc.tensor.matmul_mx(
-                    out=h_sum[:, t, :],
-                    lhsT=w1_codes[t][:].bitcast(FP8X4),
-                    lhsT_scale=w1_plane[t][:],
-                    rhs=v_words[:, cols].bitcast(FP8X4),
-                    rhs_scale=v_plane[:, cols],
-                    start=True,
-                    stop=True,
-                )
-            h_grouped = sb.tile([P, HALF, PACK], BF16, name="h_grouped%d" % u, align_bytes=64)
-            nc.scalar.activation(
-                out=h_grouped[:], in_=h_sum[:].rearrange("p t s -> p s t"), func=ACT.Relu, bias=zero[:]
+        def first_product(u, t, sums):
+            nc.tensor.matmul_mx(
+                out=sums,
+                lhsT=w1_codes[t][:].bitcast(FP8X4),
+                lhsT_scale=w1_plane[t][:],
+                rhs=v_words[u][:].bitcast(FP8X4),
+                rhs_scale=v_plane[:, u * HALF : (u + 1) * HALF],
+                start=True,
+                stop=True,
             )
+
+        def quantize_h(u, grouped):
+            cols = slice(u * HALF, (u + 1) * HALF)
             nc.vector.quantize_mx(
                 out=h_codes[:, cols].bitcast(FP8X4),
                 scales=h_plane[:, cols],
-                in_=h_grouped[:].rearrange("p s t -> p (s t)"),
+                in_=grouped[:].rearrange("p s t -> p (s t)"),
             )
 
-        steps = [(0, 0, HALF), (1, 0, S), (0, HALF, S), (2, 0, S), (3, 0, S)]
-        for c, s0, s1 in steps:
-            y_sum = ps.tile([P, s1 - s0], F32, name="y_sum%d_%d" % (c, s0))
+        h_first = sb.tile([P, HALF, PACK], BF16, name="h_first", align_bytes=64)
+        pairs = [ps.tile([P, 2, HALF], F32, name="h_pair%d" % e, tag="bank%d" % e) for e in range(2)]
+        for t in range(PACK):
+            first_product(0, t, pairs[t // 2][:, t % 2, :])
+        nc.vector.tensor_scalar_max(out=h_first[:, :, 0:2], in0=pairs[0][:].rearrange("p t s -> p s t"), scalar1=0.0)
+        nc.scalar.activation(
+            out=h_first[:, :, 2:4], in_=pairs[1][:].rearrange("p t s -> p s t"), func=ACT.Relu, bias=zero[:]
+        )
+        quantize_h(0, h_first)
+
+        h_second = sb.tile([P, HALF, PACK], BF16, name="h_second", align_bytes=64)
+        h_sum = ps.tile([P, PACK, HALF], F32, name="h_sum")
+        for t in range(PACK):
+            first_product(1, t, h_sum[:, t, :])
+        nc.scalar.activation(out=h_second[:], in_=h_sum[:].rearrange("p t s -> p s t"), func=ACT.Relu, bias=zero[:])
+        quantize_h(1, h_second)
+
+        steps = [(0, 0, HALF), (1, 0, HALF), (0, HALF, S), (1, HALF, S), (2, 0, S), (3, 0, S)]
+        for n, (c, s0, s1) in enumerate(steps):
+            y_sum = ps.tile([P, s1 - s0], F32, name="y_sum%d" % n, tag="bank%d" % ((n + 2) % 6))
             nc.tensor.matmul_mx(
                 out=y_sum[:],
                 lhsT=w2_codes[:, 2 * P * c : 2 * P * (c + 1)].bitcast(FP4X4),

from contextlib import ExitStack

import concourse.mybir as mybir

K, R, M, T, S = 512, 512, 512, 512, 256
FLOPS = 2 * K * R * S + 2 * R * M * S

F32 = mybir.dt.float32
BF16 = mybir.dt.bfloat16
I32 = mybir.dt.int32
U32 = mybir.dt.uint32
U16 = mybir.dt.uint16
U8 = mybir.dt.uint8
FP8X4 = mybir.dt.float8_e4m3fn_x4
FP4X4 = mybir.dt.float4_e2m1fn_x4
ACT = mybir.ActivationFunctionType
MULT = mybir.AluOpType.mult

P = 128
PACK = 4
HALF = S // 2


def load_scale_rows(nc, plane, rows):
    for q in range(4):
        nc.sync.dma_start(out=plane[32 * q : 32 * q + 4, :].bitcast(I32), in_=rows[4 * q : 4 * q + 4, :].bitcast(I32))


def tile_list_tabhs_m_silu_kernel(tc, tab, w1, w2_words, w2_scales, b, wgo, offs, offs2, out):
    nc = tc.nc
    with ExitStack() as ctx:
        sb = ctx.enter_context(tc.tile_pool(name="sb", bufs=1))
        ps = ctx.enter_context(tc.psum_pool(name="ps", bufs=1))

        pick = sb.tile([P, S // 16], U16, name="pick")
        place = sb.tile([P, S // 16], U16, name="place")
        tab_words = sb.tile([P, T], I32, name="tab_words", align_bytes=64)
        tab_plane = sb.tile([P, T], U8, name="tab_plane", align_bytes=64)
        w2_codes = sb.tile([P, 2 * M], U8, name="w2_codes", align_bytes=64)
        w2_plane = sb.tile([P, M], U8, name="w2_plane", align_bytes=64)
        bias = sb.tile([P, M // P], F32, name="bias")
        gain = sb.tile([P, S], F32, name="gain")
        zero_in = sb.tile([P, 1], F32, name="zero_in")
        zero = sb.tile([P, 1], F32, name="zero")
        pages = [sb.tile([P, T], F32, name="page%d" % c) for c in range(M // P)]

        nc.gpsimd.memset(zero_in[:], 0.0)
        nc.scalar.activation(out=zero[:], in_=zero_in[:], func=ACT.Silu)

        nc.vector.memset(tab_plane[:].bitcast(I32), 0)
        nc.vector.memset(w2_plane[:].bitcast(I32), 0)
        for page in pages:
            nc.vector.memset(page[:], 0.0)

        nc.sync.dma_start(pick[:], offs)
        nc.sync.dma_start(place[:], offs2)
        nc.sync.dma_start(out=tab_words[:], in_=tab[0, 0 : 4 * P * T].rearrange("(p c) -> p c", p=P).bitcast(I32))
        load_scale_rows(nc, tab_plane, tab[0, 4 * P * T :].rearrange("(q t) -> q t", t=T))
        w1_rows = w1.rearrange("(p j) r -> p j r", j=PACK)
        chunks = [(0, 256), (256, 384), (384, 512)]
        raw = []
        for n, (lo, hi) in enumerate(chunks):
            piece = sb.tile([P, PACK, hi - lo], F32, name="w1_raw%d" % n, tag="raw%d" % n, align_bytes=64)
            nc.sync.dma_start(out=piece[:], in_=w1_rows[:, :, lo:hi])
            raw.append(piece)
        nc.sync.dma_start(out=w2_codes[:].bitcast(I32), in_=w2_words[0].bitcast(I32))
        load_scale_rows(nc, w2_plane, w2_scales[0])
        with nc.allow_non_contiguous_dma(reason="one bias value a partition and row block"):
            nc.sync.dma_start(out=bias[:], in_=b.rearrange("(c p) -> p c", p=P))
        nc.sync.dma_start(out=gain[:], in_=wgo)

        def gather_words(u, tag):
            words = sb.tile([P, HALF], U32, name="v_words%d" % u, tag=tag, align_bytes=64)
            entries = pick[:, u * HALF // 16 : (u + 1) * HALF // 16]
            nc.vector.tensor_copy(out=words[:], in_=tab_words[:].bitcast(U32).indirect(entries))
            return words

        v_words = [gather_words(0, "v_words0")]
        v_plane = sb.tile([P, S], U8, name="v_plane", align_bytes=64)
        nc.vector.tensor_copy(out=v_plane[:], in_=tab_plane[:].indirect(pick[:]))

        low = sb.tile([P, PACK, 64, PACK], BF16, name="w1_low", align_bytes=64)
        high = [sb.tile([P, 2, 64, PACK], BF16, name="w1_high%d" % e, tag="high%d" % e, align_bytes=64) for e in range(2)]
        w1_codes = [sb.tile([P, P], U32, name="w1_codes%d" % t, align_bytes=64) for t in range(PACK)]
        w1_plane = [sb.tile([P, P], U8, name="w1_plane%d" % t, align_bytes=64) for t in range(PACK)]

        def source(n, m0, m1, t0, t1):
            return raw[n][:, :, PACK * m0 : PACK * m1].rearrange("p j (m t) -> p m t j", t=PACK)[:, :, t0:t1, :]

        def target(tile, m0, m1, t0, t1):
            return tile[:, t0:t1, m0:m1, :].rearrange("p t m j -> p m t j")

        def quantize_w1(u, t, rows):
            nc.vector.quantize_mx(
                out=w1_codes[t][:, 64 * u : 64 * u + 64].bitcast(FP8X4),
                scales=w1_plane[t][:, 64 * u : 64 * u + 64],
                in_=rows.rearrange("p m j -> p (m j)"),
            )

        nc.vector.tensor_copy(out=target(low, 0, 40, 0, 4), in_=source(0, 0, 40, 0, 4))
        nc.scalar.copy(out=target(low, 40, 64, 0, 4), in_=source(0, 40, 64, 0, 4))
        for t in range(PACK):
            quantize_w1(0, t, low[:, t, :, :])
        for n in (1, 2):
            m0 = 32 * (n - 1)
            nc.vector.tensor_copy(out=target(high[0], m0, m0 + 32, 0, 2), in_=source(n, 0, 32, 0, 2))
            nc.scalar.copy(out=target(high[1], m0, m0 + 32, 0, 2), in_=source(n, 0, 32, 2, 4))
        for t in range(PACK):
            quantize_w1(1, t, high[t // 2][:, t % 2, :, :])

        v_words.append(gather_words(1, "high0"))

        h_codes = sb.tile([P, S], U32, name="h_codes", align_bytes=64)
        h_plane = sb.tile([P, S], U8, name="h_plane", align_bytes=64)
        def first_product(u, t, sums):
            nc.tensor.matmul_mx(
                out=sums,
                lhsT=w1_codes[t][:].bitcast(FP8X4),
                lhsT_scale=w1_plane[t][:],
                rhs=v_words[u][:].bitcast(FP8X4),
                rhs_scale=v_plane[:, u * HALF : (u + 1) * HALF],
                start=True,
                stop=True,
            )

        def quantize_h(u, grouped):
            cols = slice(u * HALF, (u + 1) * HALF)
            nc.vector.quantize_mx(
                out=h_codes[:, cols].bitcast(FP8X4),
                scales=h_plane[:, cols],
                in_=grouped[:].rearrange("p s t -> p (s t)"),
            )

        h_first = sb.tile([P, HALF, PACK], BF16, name="h_first", align_bytes=64)
        pairs = [ps.tile([P, 2, HALF], F32, name="h_pair%d" % e, tag="bank%d" % e) for e in range(2)]
        for t in range(PACK):
            first_product(0, t, pairs[t // 2][:, t % 2, :])
        nc.vector.tensor_scalar_max(out=h_first[:, :, 0:2], in0=pairs[0][:].rearrange("p t s -> p s t"), scalar1=0.0)
        nc.scalar.activation(
            out=h_first[:, :, 2:4], in_=pairs[1][:].rearrange("p t s -> p s t"), func=ACT.Relu, bias=zero[:]
        )
        quantize_h(0, h_first)

        h_second = sb.tile([P, HALF, PACK], BF16, name="h_second", align_bytes=64)
        h_sum = ps.tile([P, PACK, HALF], F32, name="h_sum")
        for t in range(PACK):
            first_product(1, t, h_sum[:, t, :])
        nc.scalar.activation(out=h_second[:], in_=h_sum[:].rearrange("p t s -> p s t"), func=ACT.Relu, bias=zero[:])
        quantize_h(1, h_second)

        steps = [(0, 0, HALF), (1, 0, HALF), (0, HALF, S), (1, HALF, S), (2, 0, S), (3, 0, S)]
        for n, (c, s0, s1) in enumerate(steps):
            y_sum = ps.tile([P, s1 - s0], F32, name="y_sum%d" % n, tag="bank%d" % ((n + 2) % 6))
            nc.tensor.matmul_mx(
                out=y_sum[:],
                lhsT=w2_codes[:, 2 * P * c : 2 * P * (c + 1)].bitcast(FP4X4),
                lhsT_scale=w2_plane[:, P * c : P * (c + 1)],
                rhs=h_codes[:, s0:s1].bitcast(FP8X4),
                rhs_scale=h_plane[:, s0:s1],
                start=True,
                stop=True,
            )
            act = sb.tile([P, s1 - s0], F32, name="act%d_%d" % (c, s0))
            nc.scalar.activation(out=act[:], in_=y_sum[:], func=ACT.Silu, bias=bias[:, c : c + 1])
            nc.vector.tensor_tensor(
                out=pages[c][:].indirect(place[:, s0 // 16 : s1 // 16]), in0=act[:], in1=gain[:, s0:s1], op=MULT
            )
            if s1 == S:
                nc.sync.dma_start(out=out[P * c : P * (c + 1), :], in_=pages[c][:])
